import numpy as np
import ml_dtypes


def mxq(x, axis, fmt="e4m3"):
    dtype, down = {"e4m3": (ml_dtypes.float8_e4m3fn, 7), "e5m2": (ml_dtypes.float8_e5m2, 14)}[fmt]
    v = np.moveaxis(np.asarray(x, np.float32).astype(ml_dtypes.bfloat16).astype(np.float64), axis, -1)
    blocks = v.reshape(v.shape[:-1] + (-1, 32))
    amax = np.abs(blocks).max(-1, keepdims=True)
    byte = np.maximum(np.where(amax > 0, np.frexp(amax)[1] - 1 + 127, 0) - down, 1)
    scale = np.exp2(byte - 127.0)
    codes = (blocks / scale).astype(np.float32).astype(dtype).astype(np.float64)
    return np.moveaxis((codes * scale).reshape(v.shape), -1, axis)


WIDE = False


def mx_kscale(k):
    if not WIDE:
        return np.ones(k)
    levels = np.array([30, -30])
    if k % 512:
        return np.exp2(np.random.permutation(np.resize(levels, k // 32))).repeat(32)
    a = np.empty((k // 512, 16))
    for p in range(k // 512):
        a[p, :8] = np.random.permutation(np.resize(levels, 8))
        for g in range(8):
            far = levels[np.abs(levels - a[p, g]) >= 10]
            a[p, g + 8] = far[np.random.randint(len(far))]
    return np.exp2(a.ravel()).repeat(32)


def f64(x):
    return np.asarray(x).astype(np.float64)


def striped(idx):
    return np.tile(np.asarray(idx).reshape(-1, 16).T, (8, 1)).astype(np.uint16)


def unstriped(offs):
    return offs[:16].T.reshape(-1).astype(np.int64)


E2M1 = np.array([0.0, 0.5, 1.0, 1.5, 2.0, 3.0, 4.0, 6.0, -0.0, -0.5, -1.0, -1.5, -2.0, -3.0, -4.0, -6.0])


def pack_weight(w, fmt):
    k, n = w.shape
    w = f64(np.asarray(w, np.float32).astype(ml_dtypes.bfloat16)).reshape(k // 32, 32, n)
    amax = np.abs(w).max(1)
    if fmt in ("e4m3", "e5m2"):
        byte = np.frexp(amax)[1] - 1 + 127 - (7 if fmt == "e4m3" else 14)
    else:
        mant, ex = np.frexp(amax / 6.0)
        byte = np.where(mant > 0.5, ex, ex - 1) + 127
    byte = np.clip(np.where(amax > 0, byte, 1), 1, 254)
    scaled = (w * np.exp2(127.0 - byte)[:, None, :]).reshape(k, n).astype(np.float32)
    by_word = np.ascontiguousarray(scaled.reshape(k // 512, 128, 4, n).transpose(0, 1, 3, 2))
    if fmt in ("e4m3", "e5m2"):
        words = by_word.astype(ml_dtypes.float8_e4m3fn if fmt == "e4m3" else ml_dtypes.float8_e5m2).view(np.uint8)
    else:
        c = by_word.astype(ml_dtypes.float4_e2m1fn).view(np.uint8) & 0xF
        words = (c[..., 0::2] | (c[..., 1::2] << 4)).reshape(k // 512, 128, 2 * n)
    return np.ascontiguousarray(words), np.ascontiguousarray(byte.astype(np.uint8).reshape(k // 512, 16, n))


def unpack_weight(words, scales, fmt):
    g, _, n = scales.shape
    words = np.ascontiguousarray(words).reshape(g, 128, n, -1)
    if fmt in ("e4m3", "e5m2"):
        vals = words.view(ml_dtypes.float8_e4m3fn if fmt == "e4m3" else ml_dtypes.float8_e5m2).astype(np.float64)
    else:
        nib = np.empty((g, 128, n, 4), np.uint8)
        nib[..., 0::2] = words & 0xF
        nib[..., 1::2] = words >> 4
        vals = E2M1[nib]
    vals = vals * np.repeat(np.exp2(scales.astype(np.float64) - 127.0), 8, axis=1)[..., None]
    return vals.transpose(0, 1, 3, 2).reshape(g * 512, n)


def sigmoid(v):
    return 1.0 / (1.0 + np.exp(-v))


def sgn(shape):
    return np.random.uniform(0.5, 2.0, shape) * np.where(np.random.standard_normal(shape) < 0, -1.0, 1.0)


K, T, J, R, O, N, E = 512, 1024, 256, 512, 128, 256, 1024


def setup_inputs():
    n = np.random.standard_normal
    idx = np.random.permutation(T)[:J]
    idx2 = np.random.permutation(J)[:O]
    idx3 = np.random.permutation(J)[:O]
    idx4 = np.random.permutation(J)[:O]
    idx5 = np.random.permutation(J)[:O]
    idx6 = np.random.permutation(T)[:O]
    idx7 = np.random.permutation(E)[:O]
    fk = mx_kscale(K)
    fr = mx_kscale(R)
    xtp = pack_weight(n((K, T)) / fk[:, None], "e4m3")
    wp = pack_weight(n((K, R)) * 1 / np.sqrt(K) * fk[:, None], "e2m1")
    wbp = pack_weight(n((R, N)) * 1 / np.sqrt(R) / fr[:, None], "e5m2")
    wsp = pack_weight(n((K, N)) * 1 / np.sqrt(K) * fk[:, None], "e5m2")
    return {
        "xt_words": xtp[0],
        "xt_scales": xtp[1],
        "w_words": wp[0],
        "w_scales": wp[1],
        "sa": (np.random.uniform(0.5, 1.6, (R, 1)) * fr[:, None]).astype(np.float32),
        "sb": (np.random.uniform(0.5, 1.6, (R, 1)) * fr[:, None]).astype(np.float32),
        "sg": (sgn((R, 1))).astype(np.float32),
        "bg": (np.random.uniform(-2.0, 2.0, (R, 1))).astype(np.float32),
        "sh": (sgn((R, 1))).astype(np.float32),
        "bh": (np.random.uniform(-2.0, 2.0, (R, 1))).astype(np.float32),
        "wb_words": wbp[0],
        "wb_scales": wbp[1],
        "ws_words": wsp[0],
        "ws_scales": wsp[1],
        "offs": striped(idx),
        "offs2": striped(idx2),
        "offs3": striped(idx3),
        "offs4": striped(idx4),
        "offs5": striped(idx5),
        "offs6": striped(idx6),
        "offs7": striped(idx7),
    }


def reference(xt_words, xt_scales, w_words, w_scales, sa, sb, sg, bg, sh, bh, wb_words, wb_scales, ws_words, ws_scales, offs, offs2, offs3, offs4, offs5, offs6, offs7):
    idx = unstriped(offs)
    idx2 = unstriped(offs2)
    idx3 = unstriped(offs3)
    idx4 = unstriped(offs4)
    idx5 = unstriped(offs5)
    idx6 = unstriped(offs6)
    idx7 = unstriped(offs7)
    xtu = unpack_weight(xt_words, xt_scales, "e4m3")
    wu = unpack_weight(w_words, w_scales, "e2m1")
    wbu = unpack_weight(wb_words, wb_scales, "e5m2")
    wsu = unpack_weight(ws_words, ws_scales, "e5m2")
    xtidxg = xtu[:, idx]
    a = wu.T @ xtidxg
    u1 = a[:, idx2] * f64(sa) * sigmoid(a[:, idx3] * f64(sg) + f64(bg))
    u2 = a[:, idx4] * f64(sb) * sigmoid(a[:, idx5] * f64(sh) + f64(bh))
    hid = np.maximum(u1, u2)
    hidq = mxq(hid, 0, "e4m3")
    xtidx6g = xtu[:, idx6]
    p = wbu.T @ hidq + wsu.T @ xtidx6g
    y = np.zeros((N, E))
    y[:, idx7] = p
    return y

@@ -1,0 +1,165 @@
+from contextlib import ExitStack
+
+import concourse.mybir as mybir
+
+K, T, J, R, O, N, E = 512, 1024, 256, 512, 128, 256, 1024
+FLOPS = 2 * K * R * J + 2 * R * N * O + 2 * K * N * O
+
+F32 = mybir.dt.float32
+BF16 = mybir.dt.bfloat16
+I32 = mybir.dt.int32
+U32 = mybir.dt.uint32
+U16 = mybir.dt.uint16
+U8 = mybir.dt.uint8
+E4M3 = mybir.dt.float8_e4m3fn_x4
+E5M2 = mybir.dt.float8_e5m2_x4
+E2M1 = mybir.dt.float4_e2m1fn_x4
+ACT = mybir.ActivationFunctionType
+ALU = mybir.AluOpType
+
+P = 128
+PACK = 4
+
+
+def load_scale_plane(queue, plane, scales):
+    load_scale_rows(queue, plane, scales, range(4))
+
+
+def load_scale_rows(queue, plane, scales, quadrants):
+    words = plane.shape[1] // 4
+    for q in quadrants:
+        rows = scales[0, 4 * q : 4 * q + 4, :].bitcast(I32)
+        queue.dma_start(plane[32 * q : 32 * q + 32, :].bitcast(I32), rows.unsqueeze(0).to_broadcast([8, 4, words]))
+
+
+def tile_list_gatedtwins_solo_further_scattered_kernel(
+    tc, xt_words, xt_scales, w_words, w_scales, sa, sb, sg, bg, sh, bh,
+    wb_words, wb_scales, ws_words, ws_scales,
+    offs, offs2, offs3, offs4, offs5, offs6, offs7, out,
+):
+    nc = tc.nc
+    with ExitStack() as ctx:
+        lists = ctx.enter_context(tc.tile_pool(name="lists", bufs=1))
+        keep = ctx.enter_context(tc.tile_pool(name="keep", bufs=1))
+        psum = ctx.enter_context(tc.psum_pool(name="psum", bufs=1))
+
+        def load_list(src, name):
+            tile = lists.tile(list(src.shape), U16, name=name)
+            nc.sync.dma_start(tile[:], src)
+            return tile
+
+        def load_words(queue, src, name):
+            tile = keep.tile([P, src.shape[2]], U32, name=name, align_bytes=64)
+            queue.dma_start(tile[:].bitcast(I32), src[0].rearrange("p c t -> p (c t)").bitcast(I32))
+            return tile
+
+        def load_plane(queue, src, name):
+            tile = keep.tile([P, src.shape[2]], U8, name=name, align_bytes=64)
+            load_scale_plane(queue, tile, src)
+            return tile
+
+        def load_row_values(queue, src, name):
+            tile = keep.tile([P, PACK], F32, name=name)
+            queue.dma_start(tile[:], src.rearrange("(p t) one -> p (t one)", t=PACK))
+            return tile
+
+        l1 = load_list(offs, "l1")
+        x_s = load_plane(nc.scalar, xt_scales, "x_s")
+        w_s = keep.tile([P, R], U8, name="w_s", align_bytes=64)
+        load_scale_rows(nc.sync, w_s, w_scales, (0, 1))
+        x_w = load_words(nc.sync, xt_words, "x_w")
+        w_w = keep.tile([P, R], U16, name="w_w", align_bytes=64)
+        nc.sync.dma_start(w_w[:].bitcast(I32), w_words[0].bitcast(I32))
+        load_scale_rows(nc.sync, w_s, w_scales, (2, 3))
+        l3 = load_list(offs3, "l3")
+        v_sg = load_row_values(nc.sync, sg, "v_sg")
+        v_bg = load_row_values(nc.sync, bg, "v_bg")
+        l2 = load_list(offs2, "l2")
+        v_sa = load_row_values(nc.sync, sa, "v_sa")
+        l5 = load_list(offs5, "l5")
+        v_sh = load_row_values(nc.sync, sh, "v_sh")
+        v_bh = load_row_values(nc.sync, bh, "v_bh")
+        l4 = load_list(offs4, "l4")
+        v_sb = load_row_values(nc.sync, sb, "v_sb")
+        l6 = load_list(offs6, "l6")
+        ws_w = load_words(nc.sync, ws_words, "ws_w")
+        ws_s = load_plane(nc.sync, ws_scales, "ws_s")
+        wb_w = load_words(nc.sync, wb_words, "wb_w")
+        wb_s = load_plane(nc.sync, wb_scales, "wb_s")
+        l7 = load_list(offs7, "l7")
+
+        pages = [keep.tile([P, E], F32, name="page%d" % h) for h in range(N // P)]
+        for page in pages:
+            nc.vector.memset(page[:], 0.0)
+
+        xj_s = keep.tile([P, J], U8, name="xj_s", align_bytes=64)
+        xj_w = keep.tile([P, J], U32, name="xj_w", align_bytes=64)
+        nc.vector.tensor_copy(xj_s[:], x_s[:].indirect(l1[:]))
+        nc.vector.tensor_copy(xj_w[:], x_w[:].indirect(l1[:]))
+
+        wd_w = keep.tile([P, PACK, P], U16, name="wd_w", align_bytes=64)
+        wd_s = keep.tile([P, PACK, P], U8, name="wd_s", align_bytes=64)
+        for ts in (slice(0, 1), slice(1, PACK)):
+            nc.vector.tensor_copy(wd_w[:, ts, :], w_w[:].rearrange("p (m t) -> p t m", t=PACK)[:, ts, :])
+            nc.vector.tensor_copy(wd_s[:, ts, :], w_s[:].rearrange("p (m t) -> p t m", t=PACK)[:, ts, :])
+
+        a_tiles = []
+        for t in range(PACK):
+            bank = psum.tile([P, J], F32, name="a_bank%d" % t)
+            nc.tensor.matmul_mx(
+                out=bank[:], lhsT=wd_w[:, t, :].bitcast(U8).bitcast(E2M1), lhsT_scale=wd_s[:, t, :],
+                rhs=xj_w[:].bitcast(E4M3), rhs_scale=xj_s[:], start=True, stop=True,
+            )
+            a_t = keep.tile([P, J], F32, name="a%d" % t)
+            nc.vector.tensor_copy(a_t[:], bank[:])
+            a_tiles.append(a_t)
+
+        xo_s = keep.tile([P, O], U8, name="xo_s", align_bytes=64)
+        xo_w = keep.tile([P, O], U32, name="xo_w", align_bytes=64)
+        nc.vector.tensor_copy(xo_s[:], x_s[:].indirect(l6[:]))
+        nc.vector.tensor_copy(xo_w[:], x_w[:].indirect(l6[:]))
+        p_banks = [psum.tile([P, O], F32, name="p_bank%d" % h) for h in range(N // P)]
+        for h in range(N // P):
+            cols = slice(h * P, (h + 1) * P)
+            nc.tensor.matmul_mx(
+                out=p_banks[h][:], lhsT=ws_w[:, cols].bitcast(E5M2), lhsT_scale=ws_s[:, cols],
+                rhs=xo_w[:].bitcast(E4M3), rhs_scale=xo_s[:], start=True, stop=False,
+            )
+
+        hid = keep.tile([P, O, PACK], BF16, name="hid", align_bytes=64)
+        for pair in range(PACK // 2):
+            u = keep.tile([P, 2, 2, O], F32, name="u%d" % pair)
+            for i in range(2):
+                t = 2 * pair + i
+                col = slice(t, t + 1)
+                a_t = a_tiles[t]
+                for twin, (lv, lg, wt, sl, bi) in enumerate(((l2, l3, v_sa, v_sg, v_bg), (l4, l5, v_sb, v_sh, v_bh))):
+                    gate = keep.tile([P, O], F32, name="gate%d_%d" % (t, twin))
+                    val = keep.tile([P, O], F32, name="val%d_%d" % (t, twin))
+                    nc.scalar.activation(gate[:], a_t[:].indirect(lg[:]), ACT.Sigmoid, bias=bi[:, col], scale=sl[:, col])
+                    nc.scalar.activation(val[:], a_t[:].indirect(lv[:]), ACT.Copy, scale=wt[:, col])
+                    nc.vector.tensor_tensor(u[:, twin, i, :], val[:], gate[:], ALU.mult)
+            nc.vector.tensor_tensor(
+                hid[:, :, 2 * pair : 2 * pair + 2],
+                u[:, 0].rearrange("p i o -> p o i"), u[:, 1].rearrange("p i o -> p o i"), ALU.max,
+            )
+
+        hq_w = keep.tile([P, O], U32, name="hq_w", align_bytes=64)
+        hq_s = keep.tile([P, O], U8, name="hq_s", align_bytes=64)
+        nc.vector.quantize_mx(out=hq_w[:].bitcast(E4M3), scales=hq_s[:], in_=hid[:].rearrange("p o t -> p (o t)"))
+
+        for h in range(N // P):
+            cols = slice(h * P, (h + 1) * P)
+            nc.tensor.matmul_mx(
+                out=p_banks[h][:], lhsT=wb_w[:, cols].bitcast(E5M2), lhsT_scale=wb_s[:, cols],
+                rhs=hq_w[:].bitcast(E4M3), rhs_scale=hq_s[:], start=False, stop=True,
+            )
+            p_sb = keep.tile([P, O], F32, name="p_sb%d" % h)
+            if h == 0:
+                nc.vector.tensor_copy(p_sb[:], p_banks[h][:])
+                nc.vector.tensor_copy(pages[h][:].indirect(l7[:]), p_sb[:])
+                nc.sync.dma_start(out[cols, :], pages[h][:])
+            else:
+                nc.scalar.copy(p_sb[:], p_banks[h][:])
+                nc.scalar.activation(pages[h][:].indirect(l7[:]), p_sb[:], ACT.Copy)
+                nc.scalar.dma_start(out[cols, :], pages[h][:])

@@ -88,6 +88,10 @@ def tile_list_gatedtwins_solo_further_scattered_kernel(
         wb_s = load_plane(nc.sync, wb_scales, "wb_s")
         l7 = load_list(offs7, "l7")
 
+        warm = keep.tile([P, 2], F32, name="warm")
+        nc.gpsimd.memset(warm[:, 0:1], 0.0)
+        nc.scalar.activation(warm[:, 1:2], warm[:, 0:1], ACT.Sigmoid)
+
         pages = [keep.tile([P, E], F32, name="page%d" % h) for h in range(N // P)]
         for page in pages:
             nc.vector.memset(page[:], 0.0)

@@ -49,7 +49,7 @@ def tile_list_gatedtwins_solo_further_scattered_kernel(
             return tile
 
         def load_words(queue, src, name):
-            tile = keep.tile([P, src.shape[2]], U32, name=name, align_bytes=64)
+            tile = keep.tile([P, src.shape[2]], U32, name=name, tag=name, align_bytes=64)
             queue.dma_start(tile[:].bitcast(I32), src[0].rearrange("p c t -> p (c t)").bitcast(I32))
             return tile
 
@@ -64,13 +64,16 @@ def tile_list_gatedtwins_solo_further_scattered_kernel(
             return tile
 
         l1 = load_list(offs, "l1")
-        x_s = load_plane(nc.scalar, xt_scales, "x_s")
-        w_s = keep.tile([P, R], U8, name="w_s", align_bytes=64)
-        load_scale_rows(nc.sync, w_s, w_scales, (0, 1))
+        x_s = keep.tile([P, T], U8, name="x_s", align_bytes=64)
+        load_scale_rows(nc.scalar, x_s, xt_scales, (0, 1, 2))
+        l6 = load_list(offs6, "l6")
+        load_scale_rows(nc.sync, x_s, xt_scales, (3,))
         x_w = load_words(nc.sync, xt_words, "x_w")
+        w_s = keep.tile([P, R], U8, name="w_s", align_bytes=64)
+        load_scale_rows(nc.scalar, w_s, w_scales, (0,))
         w_w = keep.tile([P, R], U16, name="w_w", align_bytes=64)
         nc.sync.dma_start(w_w[:].bitcast(I32), w_words[0].bitcast(I32))
-        load_scale_rows(nc.sync, w_s, w_scales, (2, 3))
+        load_scale_rows(nc.sync, w_s, w_scales, (1, 2, 3))
         l3 = load_list(offs3, "l3")
         v_sg = load_row_values(nc.sync, sg, "v_sg")
         v_bg = load_row_values(nc.sync, bg, "v_bg")
@@ -81,7 +84,6 @@ def tile_list_gatedtwins_solo_further_scattered_kernel(
         v_bh = load_row_values(nc.sync, bh, "v_bh")
         l4 = load_list(offs4, "l4")
         v_sb = load_row_values(nc.sync, sb, "v_sb")
-        l6 = load_list(offs6, "l6")
         ws_w = load_words(nc.sync, ws_words, "ws_w")
         ws_s = load_plane(nc.sync, ws_scales, "ws_s")
         wb_w = load_words(nc.sync, wb_words, "wb_w")
@@ -89,7 +91,7 @@ def tile_list_gatedtwins_solo_further_scattered_kernel(
         l7 = load_list(offs7, "l7")
 
         warm = keep.tile([P, 2], F32, name="warm")
-        nc.gpsimd.memset(warm[:, 0:1], 0.0)
+        nc.vector.memset(warm[:, 0:1], 0.0)
         nc.scalar.activation(warm[:, 1:2], warm[:, 0:1], ACT.Sigmoid)
 
         pages = [keep.tile([P, E], F32, name="page%d" % h) for h in range(N // P)]
@@ -98,31 +100,32 @@ def tile_list_gatedtwins_solo_further_scattered_kernel(
 
         xj_s = keep.tile([P, J], U8, name="xj_s", align_bytes=64)
         xj_w = keep.tile([P, J], U32, name="xj_w", align_bytes=64)
-        nc.vector.tensor_copy(xj_s[:], x_s[:].indirect(l1[:]))
-        nc.vector.tensor_copy(xj_w[:], x_w[:].indirect(l1[:]))
-
-        wd_w = keep.tile([P, PACK, P], U16, name="wd_w", align_bytes=64)
-        wd_s = keep.tile([P, PACK, P], U8, name="wd_s", align_bytes=64)
-        for ts in (slice(0, 1), slice(1, PACK)):
-            nc.vector.tensor_copy(wd_w[:, ts, :], w_w[:].rearrange("p (m t) -> p t m", t=PACK)[:, ts, :])
-            nc.vector.tensor_copy(wd_s[:, ts, :], w_s[:].rearrange("p (m t) -> p t m", t=PACK)[:, ts, :])
-
-        a_tiles = []
-        for t in range(PACK):
-            bank = psum.tile([P, J], F32, name="a_bank%d" % t)
-            nc.tensor.matmul_mx(
-                out=bank[:], lhsT=wd_w[:, t, :].bitcast(U8).bitcast(E2M1), lhsT_scale=wd_s[:, t, :],
-                rhs=xj_w[:].bitcast(E4M3), rhs_scale=xj_s[:], start=True, stop=True,
-            )
-            a_t = keep.tile([P, J], F32, name="a%d" % t)
-            nc.vector.tensor_copy(a_t[:], bank[:])
-            a_tiles.append(a_t)
-
         xo_s = keep.tile([P, O], U8, name="xo_s", align_bytes=64)
         xo_w = keep.tile([P, O], U32, name="xo_w", align_bytes=64)
+        nc.vector.tensor_copy(xj_s[:], x_s[:].indirect(l1[:]))
         nc.vector.tensor_copy(xo_s[:], x_s[:].indirect(l6[:]))
+        halves = (slice(0, J // 2), slice(J // 2, J))
+        nc.vector.tensor_copy(xj_w[:], x_w[:].indirect(l1[:]))
         nc.vector.tensor_copy(xo_w[:], x_w[:].indirect(l6[:]))
-        p_banks = [psum.tile([P, O], F32, name="p_bank%d" % h) for h in range(N // P)]
+
+        wd_w = keep.tile([P, PACK, P], U16, name="wd_w", align_bytes=64)
+        wd_s = keep.tile([P, PACK, P], U8, name="wd_s", tag="x_w", align_bytes=64)
+        for ts in (slice(0, 1), slice(1, PACK)):
+            nc.vector.tensor_copy(wd_s[:, ts, :], w_s[:].rearrange("p (m t) -> p t m", t=PACK)[:, ts, :])
+            nc.scalar.copy(wd_w[:, ts, :], w_w[:].rearrange("p (m t) -> p t m", t=PACK)[:, ts, :])
+
+        a_tiles = [keep.tile([P, J], F32, name="a%d" % t) for t in range(PACK)]
+        pieces = [(0, halves[0], nc.scalar.copy), (0, halves[1], nc.vector.tensor_copy)]
+        pieces.extend((t, slice(0, J), nc.vector.tensor_copy) for t in range(1, PACK))
+        for i, (t, cols, copy_out) in enumerate(pieces):
+            bank = psum.tile([P, cols.stop - cols.start], F32, name="a_bank%d" % i, tag="bank%d" % i)
+            nc.tensor.matmul_mx(
+                out=bank[:], lhsT=wd_w[:, t, :].bitcast(U8).bitcast(E2M1), lhsT_scale=wd_s[:, t, :],
+                rhs=xj_w[:, cols].bitcast(E4M3), rhs_scale=xj_s[:, cols], start=True, stop=True,
+            )
+            copy_out(a_tiles[t][:, cols], bank[:])
+
+        p_banks = [psum.tile([P, O], F32, name="p_bank%d" % h, tag="bank%d" % (3 + h)) for h in range(N // P)]
         for h in range(N // P):
             cols = slice(h * P, (h + 1) * P)
             nc.tensor.matmul_mx(
@@ -131,26 +134,46 @@ def tile_list_gatedtwins_solo_further_scattered_kernel(
             )
 
         hid = keep.tile([P, O, PACK], BF16, name="hid", align_bytes=64)
-        for pair in range(PACK // 2):
-            u = keep.tile([P, 2, 2, O], F32, name="u%d" % pair)
-            for i in range(2):
-                t = 2 * pair + i
-                col = slice(t, t + 1)
-                a_t = a_tiles[t]
-                for twin, (lv, lg, wt, sl, bi) in enumerate(((l2, l3, v_sa, v_sg, v_bg), (l4, l5, v_sb, v_sh, v_bh))):
-                    gate = keep.tile([P, O], F32, name="gate%d_%d" % (t, twin))
-                    val = keep.tile([P, O], F32, name="val%d_%d" % (t, twin))
-                    nc.scalar.activation(gate[:], a_t[:].indirect(lg[:]), ACT.Sigmoid, bias=bi[:, col], scale=sl[:, col])
-                    nc.scalar.activation(val[:], a_t[:].indirect(lv[:]), ACT.Copy, scale=wt[:, col])
-                    nc.vector.tensor_tensor(u[:, twin, i, :], val[:], gate[:], ALU.mult)
-            nc.vector.tensor_tensor(
-                hid[:, :, 2 * pair : 2 * pair + 2],
-                u[:, 0].rearrange("p i o -> p o i"), u[:, 1].rearrange("p i o -> p o i"), ALU.max,
-            )
-
         hq_w = keep.tile([P, O], U32, name="hq_w", align_bytes=64)
         hq_s = keep.tile([P, O], U8, name="hq_s", align_bytes=64)
-        nc.vector.quantize_mx(out=hq_w[:].bitcast(E4M3), scales=hq_s[:], in_=hid[:].rearrange("p o t -> p (o t)"))
+        twins = ((l2, l3, v_sa, v_sg, v_bg), (l4, l5, v_sb, v_sh, v_bh))
+        u = keep.tile([P, 2, PACK, O], F32, name="u")
+        whole = (slice(0, O),)
+        in_halves = (slice(0, O // 2), slice(O // 2, O))
+
+        def look(t, entries, places, func, name, **affine):
+            picked = keep.tile([P, places.stop - places.start], F32, name="%s%d_%d" % (name, t, places.start))
+            columns = {key: tile[:, t : t + 1] for key, tile in affine.items()}
+            window = a_tiles[t][:].indirect(entries[:, places.start // 16 : places.stop // 16])
+            nc.scalar.activation(picked[:], window, func, **columns)
+            return picked
+
+        def gated(ts, twin, places):
+            lv, lg, wt, sl, bi = twins[twin]
+            gates = [look(t, lg, places, ACT.Sigmoid, "gate%d" % twin, bias=bi, scale=sl) for t in ts]
+            for t, gate in zip(ts, gates):
+                val = look(t, lv, places, ACT.Copy, "val%d" % twin, scale=wt)
+                nc.vector.tensor_tensor(u[:, twin, t, places], val[:], gate[:], ALU.mult)
+
+        def larger(pair, places):
+            ts = slice(2 * pair, 2 * pair + 2)
+            nc.vector.tensor_tensor(
+                hid[:, places, ts],
+                u[:, 0, ts, places].rearrange("p t o -> p o t"), u[:, 1, ts, places].rearrange("p t o -> p o t"), ALU.max,
+            )
+
+        for pair in range(2):
+            gated((2 * pair, 2 * pair + 1), 0, slice(0, O))
+        gated((0, 1), 1, slice(0, O))
+        larger(0, slice(0, O))
+        gated((2,), 1, slice(0, O))
+        for places in in_halves:
+            gated((3,), 1, places)
+            larger(1, places)
+            nc.vector.quantize_mx(
+                out=hq_w[:, places].bitcast(E4M3), scales=hq_s[:, places],
+                in_=hid[:, places, :].rearrange("p o t -> p (o t)"),
+            )
 
         for h in range(N // P):
             cols = slice(h * P, (h + 1) * P)

@@ -66,24 +66,24 @@ def tile_list_gatedtwins_solo_further_scattered_kernel(
         l1 = load_list(offs, "l1")
         x_s = keep.tile([P, T], U8, name="x_s", align_bytes=64)
         load_scale_rows(nc.scalar, x_s, xt_scales, (0, 1, 2))
-        l6 = load_list(offs6, "l6")
         load_scale_rows(nc.sync, x_s, xt_scales, (3,))
-        x_w = load_words(nc.sync, xt_words, "x_w")
         w_s = keep.tile([P, R], U8, name="w_s", align_bytes=64)
-        load_scale_rows(nc.scalar, w_s, w_scales, (0,))
+        load_scale_rows(nc.sync, w_s, w_scales, (0,))
+        x_w = load_words(nc.sync, xt_words, "x_w")
         w_w = keep.tile([P, R], U16, name="w_w", align_bytes=64)
-        nc.sync.dma_start(w_w[:].bitcast(I32), w_words[0].bitcast(I32))
+        nc.scalar.dma_start(w_w[:].bitcast(I32), w_words[0].bitcast(I32))
         load_scale_rows(nc.sync, w_s, w_scales, (1, 2, 3))
+        l2 = load_list(offs2, "l2")
+        v_sa = load_row_values(nc.sync, sa, "v_sa")
+        l4 = load_list(offs4, "l4")
+        v_sb = load_row_values(nc.sync, sb, "v_sb")
         l3 = load_list(offs3, "l3")
         v_sg = load_row_values(nc.sync, sg, "v_sg")
         v_bg = load_row_values(nc.sync, bg, "v_bg")
-        l2 = load_list(offs2, "l2")
-        v_sa = load_row_values(nc.sync, sa, "v_sa")
         l5 = load_list(offs5, "l5")
         v_sh = load_row_values(nc.sync, sh, "v_sh")
         v_bh = load_row_values(nc.sync, bh, "v_bh")
-        l4 = load_list(offs4, "l4")
-        v_sb = load_row_values(nc.sync, sb, "v_sb")
+        l6 = load_list(offs6, "l6")
         ws_w = load_words(nc.sync, ws_words, "ws_w")
         ws_s = load_plane(nc.sync, ws_scales, "ws_s")
         wb_w = load_words(nc.sync, wb_words, "wb_w")
@@ -98,18 +98,14 @@ def tile_list_gatedtwins_solo_further_scattered_kernel(
         for page in pages:
             nc.vector.memset(page[:], 0.0)
 
-        xj_s = keep.tile([P, J], U8, name="xj_s", align_bytes=64)
-        xj_w = keep.tile([P, J], U32, name="xj_w", align_bytes=64)
-        xo_s = keep.tile([P, O], U8, name="xo_s", align_bytes=64)
-        xo_w = keep.tile([P, O], U32, name="xo_w", align_bytes=64)
+        xj_s = keep.tile([P, J], U8, name="xj_s", tag="picked_scales", align_bytes=64)
+        xj_w = keep.tile([P, J], U32, name="xj_w", tag="picked_words", align_bytes=64)
         nc.vector.tensor_copy(xj_s[:], x_s[:].indirect(l1[:]))
-        nc.vector.tensor_copy(xo_s[:], x_s[:].indirect(l6[:]))
         halves = (slice(0, J // 2), slice(J // 2, J))
         nc.vector.tensor_copy(xj_w[:], x_w[:].indirect(l1[:]))
-        nc.vector.tensor_copy(xo_w[:], x_w[:].indirect(l6[:]))
 
         wd_w = keep.tile([P, PACK, P], U16, name="wd_w", align_bytes=64)
-        wd_s = keep.tile([P, PACK, P], U8, name="wd_s", tag="x_w", align_bytes=64)
+        wd_s = keep.tile([P, PACK, P], U8, name="wd_s", align_bytes=64)
         for ts in (slice(0, 1), slice(1, PACK)):
             nc.vector.tensor_copy(wd_s[:, ts, :], w_s[:].rearrange("p (m t) -> p t m", t=PACK)[:, ts, :])
             nc.scalar.copy(wd_w[:, ts, :], w_w[:].rearrange("p (m t) -> p t m", t=PACK)[:, ts, :])
@@ -125,6 +121,10 @@ def tile_list_gatedtwins_solo_further_scattered_kernel(
             )
             copy_out(a_tiles[t][:, cols], bank[:])
 
+        xo_s = keep.tile([P, O], U8, name="xo_s", tag="picked_scales", align_bytes=64)
+        nc.vector.tensor_copy(xo_s[:], x_s[:].indirect(l6[:]))
+        xo_w = keep.tile([P, O], U32, name="xo_w", tag="picked_words", align_bytes=64)
+        nc.vector.tensor_copy(xo_w[:], x_w[:].indirect(l6[:]))
         p_banks = [psum.tile([P, O], F32, name="p_bank%d" % h, tag="bank%d" % (3 + h)) for h in range(N // P)]
         for h in range(N // P):
             cols = slice(h * P, (h + 1) * P)
@@ -148,11 +148,11 @@ def tile_list_gatedtwins_solo_further_scattered_kernel(
             nc.scalar.activation(picked[:], window, func, **columns)
             return picked
 
-        def gated(ts, twin, places):
-            lv, lg, wt, sl, bi = twins[twin]
-            gates = [look(t, lg, places, ACT.Sigmoid, "gate%d" % twin, bias=bi, scale=sl) for t in ts]
-            for t, gate in zip(ts, gates):
-                val = look(t, lv, places, ACT.Copy, "val%d" % twin, scale=wt)
+        def gated(ts, which, places):
+            looks = [(t, twin) for t in ts for twin in which]
+            vals = [look(t, twins[twin][0], places, ACT.Copy, "val%d" % twin, scale=twins[twin][2]) for t, twin in looks]
+            for (t, twin), val in zip(looks, vals):
+                gate = look(t, twins[twin][1], places, ACT.Sigmoid, "gate%d" % twin, scale=twins[twin][3], bias=twins[twin][4])
                 nc.vector.tensor_tensor(u[:, twin, t, places], val[:], gate[:], ALU.mult)
 
         def larger(pair, places):
@@ -162,13 +162,12 @@ def tile_list_gatedtwins_solo_further_scattered_kernel(
                 u[:, 0, ts, places].rearrange("p t o -> p o t"), u[:, 1, ts, places].rearrange("p t o -> p o t"), ALU.max,
             )
 
-        for pair in range(2):
-            gated((2 * pair, 2 * pair + 1), 0, slice(0, O))
-        gated((0, 1), 1, slice(0, O))
+        gated((0, 1), (0, 1), slice(0, O))
         larger(0, slice(0, O))
-        gated((2,), 1, slice(0, O))
+        gated((2,), (0, 1), slice(0, O))
+        gated((3,), (0,), slice(0, O))
         for places in in_halves:
-            gated((3,), 1, places)
+            gated((3,), (1,), places)
             larger(1, places)
             nc.vector.quantize_mx(
                 out=hq_w[:, places].bitcast(E4M3), scales=hq_s[:, places],

from contextlib import ExitStack

import concourse.mybir as mybir

K, T, J, R, O, N, E = 512, 1024, 256, 512, 128, 256, 1024
FLOPS = 2 * K * R * J + 2 * R * N * O + 2 * K * N * O

F32 = mybir.dt.float32
BF16 = mybir.dt.bfloat16
I32 = mybir.dt.int32
U32 = mybir.dt.uint32
U16 = mybir.dt.uint16
U8 = mybir.dt.uint8
E4M3 = mybir.dt.float8_e4m3fn_x4
E5M2 = mybir.dt.float8_e5m2_x4
E2M1 = mybir.dt.float4_e2m1fn_x4
ACT = mybir.ActivationFunctionType
ALU = mybir.AluOpType

P = 128
PACK = 4


def load_scale_plane(queue, plane, scales):
    load_scale_rows(queue, plane, scales, range(4))


def load_scale_rows(queue, plane, scales, quadrants):
    words = plane.shape[1] // 4
    for q in quadrants:
        rows = scales[0, 4 * q : 4 * q + 4, :].bitcast(I32)
        queue.dma_start(plane[32 * q : 32 * q + 32, :].bitcast(I32), rows.unsqueeze(0).to_broadcast([8, 4, words]))


def tile_list_gatedtwins_solo_further_scattered_kernel(
    tc, xt_words, xt_scales, w_words, w_scales, sa, sb, sg, bg, sh, bh,
    wb_words, wb_scales, ws_words, ws_scales,
    offs, offs2, offs3, offs4, offs5, offs6, offs7, out,
):
    nc = tc.nc
    with ExitStack() as ctx:
        lists = ctx.enter_context(tc.tile_pool(name="lists", bufs=1))
        keep = ctx.enter_context(tc.tile_pool(name="keep", bufs=1))
        psum = ctx.enter_context(tc.psum_pool(name="psum", bufs=1))

        def load_list(src, name):
            tile = lists.tile(list(src.shape), U16, name=name)
            nc.sync.dma_start(tile[:], src)
            return tile

        def load_words(queue, src, name):
            tile = keep.tile([P, src.shape[2]], U32, name=name, tag=name, align_bytes=64)
            queue.dma_start(tile[:].bitcast(I32), src[0].rearrange("p c t -> p (c t)").bitcast(I32))
            return tile

        def load_plane(queue, src, name):
            tile = keep.tile([P, src.shape[2]], U8, name=name, align_bytes=64)
            load_scale_plane(queue, tile, src)
            return tile

        def load_row_values(queue, src, name):
            tile = keep.tile([P, PACK], F32, name=name)
            queue.dma_start(tile[:], src.rearrange("(p t) one -> p (t one)", t=PACK))
            return tile

        l1 = load_list(offs, "l1")
        x_s = keep.tile([P, T], U8, name="x_s", align_bytes=64)
        load_scale_rows(nc.scalar, x_s, xt_scales, (0, 1, 2))
        load_scale_rows(nc.sync, x_s, xt_scales, (3,))
        w_s = keep.tile([P, R], U8, name="w_s", align_bytes=64)
        load_scale_rows(nc.sync, w_s, w_scales, (0,))
        x_w = load_words(nc.sync, xt_words, "x_w")
        w_w = keep.tile([P, R], U16, name="w_w", align_bytes=64)
        nc.scalar.dma_start(w_w[:].bitcast(I32), w_words[0].bitcast(I32))
        load_scale_rows(nc.sync, w_s, w_scales, (1, 2, 3))
        l2 = load_list(offs2, "l2")
        v_sa = load_row_values(nc.sync, sa, "v_sa")
        l4 = load_list(offs4, "l4")
        v_sb = load_row_values(nc.sync, sb, "v_sb")
        l3 = load_list(offs3, "l3")
        v_sg = load_row_values(nc.sync, sg, "v_sg")
        v_bg = load_row_values(nc.sync, bg, "v_bg")
        l5 = load_list(offs5, "l5")
        v_sh = load_row_values(nc.sync, sh, "v_sh")
        v_bh = load_row_values(nc.sync, bh, "v_bh")
        l6 = load_list(offs6, "l6")
        ws_w = load_words(nc.sync, ws_words, "ws_w")
        ws_s = load_plane(nc.sync, ws_scales, "ws_s")
        wb_w = load_words(nc.sync, wb_words, "wb_w")
        wb_s = load_plane(nc.sync, wb_scales, "wb_s")
        l7 = load_list(offs7, "l7")

        warm = keep.tile([P, 2], F32, name="warm")
        nc.vector.memset(warm[:, 0:1], 0.0)
        nc.scalar.activation(warm[:, 1:2], warm[:, 0:1], ACT.Sigmoid)

        pages = [keep.tile([P, E], F32, name="page%d" % h) for h in range(N // P)]
        for page in pages:
            nc.vector.memset(page[:], 0.0)

        xj_s = keep.tile([P, J], U8, name="xj_s", tag="picked_scales", align_bytes=64)
        xj_w = keep.tile([P, J], U32, name="xj_w", tag="picked_words", align_bytes=64)
        nc.vector.tensor_copy(xj_s[:], x_s[:].indirect(l1[:]))
        halves = (slice(0, J // 2), slice(J // 2, J))
        nc.vector.tensor_copy(xj_w[:], x_w[:].indirect(l1[:]))

        wd_w = keep.tile([P, PACK, P], U16, name="wd_w", align_bytes=64)
        wd_s = keep.tile([P, PACK, P], U8, name="wd_s", align_bytes=64)
        for ts in (slice(0, 1), slice(1, PACK)):
            nc.vector.tensor_copy(wd_s[:, ts, :], w_s[:].rearrange("p (m t) -> p t m", t=PACK)[:, ts, :])
            nc.scalar.copy(wd_w[:, ts, :], w_w[:].rearrange("p (m t) -> p t m", t=PACK)[:, ts, :])

        a_tiles = [keep.tile([P, J], F32, name="a%d" % t) for t in range(PACK)]
        pieces = [(0, halves[0], nc.scalar.copy), (0, halves[1], nc.vector.tensor_copy)]
        pieces.extend((t, slice(0, J), nc.vector.tensor_copy) for t in range(1, PACK))
        for i, (t, cols, copy_out) in enumerate(pieces):
            bank = psum.tile([P, cols.stop - cols.start], F32, name="a_bank%d" % i, tag="bank%d" % i)
            nc.tensor.matmul_mx(
                out=bank[:], lhsT=wd_w[:, t, :].bitcast(U8).bitcast(E2M1), lhsT_scale=wd_s[:, t, :],
                rhs=xj_w[:, cols].bitcast(E4M3), rhs_scale=xj_s[:, cols], start=True, stop=True,
            )
            copy_out(a_tiles[t][:, cols], bank[:])

        xo_s = keep.tile([P, O], U8, name="xo_s", tag="picked_scales", align_bytes=64)
        nc.vector.tensor_copy(xo_s[:], x_s[:].indirect(l6[:]))
        xo_w = keep.tile([P, O], U32, name="xo_w", tag="picked_words", align_bytes=64)
        nc.vector.tensor_copy(xo_w[:], x_w[:].indirect(l6[:]))
        p_banks = [psum.tile([P, O], F32, name="p_bank%d" % h, tag="bank%d" % (3 + h)) for h in range(N // P)]
        for h in range(N // P):
            cols = slice(h * P, (h + 1) * P)
            nc.tensor.matmul_mx(
                out=p_banks[h][:], lhsT=ws_w[:, cols].bitcast(E5M2), lhsT_scale=ws_s[:, cols],
                rhs=xo_w[:].bitcast(E4M3), rhs_scale=xo_s[:], start=True, stop=False,
            )

        hid = keep.tile([P, O, PACK], BF16, name="hid", align_bytes=64)
        hq_w = keep.tile([P, O], U32, name="hq_w", align_bytes=64)
        hq_s = keep.tile([P, O], U8, name="hq_s", align_bytes=64)
        twins = ((l2, l3, v_sa, v_sg, v_bg), (l4, l5, v_sb, v_sh, v_bh))
        u = keep.tile([P, 2, PACK, O], F32, name="u")
        whole = (slice(0, O),)
        in_halves = (slice(0, O // 2), slice(O // 2, O))

        def look(t, entries, places, func, name, **affine):
            picked = keep.tile([P, places.stop - places.start], F32, name="%s%d_%d" % (name, t, places.start))
            columns = {key: tile[:, t : t + 1] for key, tile in affine.items()}
            window = a_tiles[t][:].indirect(entries[:, places.start // 16 : places.stop // 16])
            nc.scalar.activation(picked[:], window, func, **columns)
            return picked

        def gated(ts, which, places):
            looks = [(t, twin) for t in ts for twin in which]
            vals = [look(t, twins[twin][0], places, ACT.Copy, "val%d" % twin, scale=twins[twin][2]) for t, twin in looks]
            for (t, twin), val in zip(looks, vals):
                gate = look(t, twins[twin][1], places, ACT.Sigmoid, "gate%d" % twin, scale=twins[twin][3], bias=twins[twin][4])
                nc.vector.tensor_tensor(u[:, twin, t, places], val[:], gate[:], ALU.mult)

        def larger(pair, places):
            ts = slice(2 * pair, 2 * pair + 2)
            nc.vector.tensor_tensor(
                hid[:, places, ts],
                u[:, 0, ts, places].rearrange("p t o -> p o t"), u[:, 1, ts, places].rearrange("p t o -> p o t"), ALU.max,
            )

        gated((0, 1), (0, 1), slice(0, O))
        larger(0, slice(0, O))
        gated((2,), (0, 1), slice(0, O))
        gated((3,), (0,), slice(0, O))
        for places in in_halves:
            gated((3,), (1,), places)
            larger(1, places)
            nc.vector.quantize_mx(
                out=hq_w[:, places].bitcast(E4M3), scales=hq_s[:, places],
                in_=hid[:, places, :].rearrange("p o t -> p (o t)"),
            )

        for h in range(N // P):
            cols = slice(h * P, (h + 1) * P)
            nc.tensor.matmul_mx(
                out=p_banks[h][:], lhsT=wb_w[:, cols].bitcast(E5M2), lhsT_scale=wb_s[:, cols],
                rhs=hq_w[:].bitcast(E4M3), rhs_scale=hq_s[:], start=False, stop=True,
            )
            p_sb = keep.tile([P, O], F32, name="p_sb%d" % h)
            if h == 0:
                nc.vector.tensor_copy(p_sb[:], p_banks[h][:])
                nc.vector.tensor_copy(pages[h][:].indirect(l7[:]), p_sb[:])
                nc.sync.dma_start(out[cols, :], pages[h][:])
            else:
                nc.scalar.copy(p_sb[:], p_banks[h][:])
                nc.scalar.activation(pages[h][:].indirect(l7[:]), p_sb[:], ACT.Copy)
                nc.scalar.dma_start(out[cols, :], pages[h][:])
